import numpy as np
import ml_dtypes


def mxq(x, axis, fmt="e4m3"):
    dtype, down = {"e4m3": (ml_dtypes.float8_e4m3fn, 7), "e5m2": (ml_dtypes.float8_e5m2, 14)}[fmt]
    v = np.moveaxis(np.asarray(x, np.float32).astype(ml_dtypes.bfloat16).astype(np.float64), axis, -1)
    blocks = v.reshape(v.shape[:-1] + (-1, 32))
    amax = np.abs(blocks).max(-1, keepdims=True)
    byte = np.maximum(np.where(amax > 0, np.frexp(amax)[1] - 1 + 127, 0) - down, 1)
    scale = np.exp2(byte - 127.0)
    codes = (blocks / scale).astype(np.float32).astype(dtype).astype(np.float64)
    return np.moveaxis((codes * scale).reshape(v.shape), -1, axis)


WIDE = False


def mx_kscale(k):
    if not WIDE:
        return np.ones(k)
    levels = np.array([10, -10, 5, -5, 0])
    if k % 512:
        return np.exp2(np.random.permutation(np.resize(levels, k // 32))).repeat(32)
    a = np.empty((k // 512, 16))
    for p in range(k // 512):
        a[p, :8] = np.random.permutation(np.resize(levels, 8))
        for g in range(8):
            far = levels[np.abs(levels - a[p, g]) >= 10]
            a[p, g + 8] = far[np.random.randint(len(far))]
    return np.exp2(a.ravel()).repeat(32)


def f64(x):
    return np.asarray(x).astype(np.float64)


def striped(idx):
    return np.tile(idx.reshape(-1, 16).T, (8, 1)).astype(np.uint16)


def unstriped(offs):
    return offs[:16].T.reshape(-1).astype(np.int64)


E2M1 = np.array([0.0, 0.5, 1.0, 1.5, 2.0, 3.0, 4.0, 6.0, -0.0, -0.5, -1.0, -1.5, -2.0, -3.0, -4.0, -6.0])


def pack_weight(w, fmt):
    k, n = w.shape
    w = f64(np.asarray(w, np.float32).astype(ml_dtypes.bfloat16)).reshape(k // 32, 32, n)
    amax = np.abs(w).max(1)
    if fmt == "e4m3":
        byte = np.frexp(amax)[1] - 1 + 127 - 7
    else:
        mant, ex = np.frexp(amax / 6.0)
        byte = np.where(mant > 0.5, ex, ex - 1) + 127
    byte = np.clip(np.where(amax > 0, byte, 1), 1, 254)
    scaled = (w * np.exp2(127.0 - byte)[:, None, :]).reshape(k, n).astype(np.float32)
    by_word = np.ascontiguousarray(scaled.reshape(k // 512, 128, 4, n).transpose(0, 1, 3, 2))
    if fmt == "e4m3":
        words = by_word.astype(ml_dtypes.float8_e4m3fn).view(np.uint8)
    else:
        c = by_word.astype(ml_dtypes.float4_e2m1fn).view(np.uint8) & 0xF
        words = (c[..., 0::2] | (c[..., 1::2] << 4)).reshape(k // 512, 128, 2 * n)
    return np.ascontiguousarray(words), np.ascontiguousarray(byte.astype(np.uint8).reshape(k // 512, 16, n))


def unpack_weight(words, scales, fmt):
    g, _, n = scales.shape
    words = np.ascontiguousarray(words).reshape(g, 128, n, -1)
    if fmt == "e4m3":
        vals = words.view(ml_dtypes.float8_e4m3fn).astype(np.float64)
    else:
        nib = np.empty((g, 128, n, 4), np.uint8)
        nib[..., 0::2] = words & 0xF
        nib[..., 1::2] = words >> 4
        vals = E2M1[nib]
    vals = vals * np.repeat(np.exp2(scales.astype(np.float64) - 127.0), 8, axis=1)[..., None]
    return vals.transpose(0, 1, 3, 2).reshape(g * 512, n)


def gelu(v):
    return 0.5 * v * (1.0 + np.tanh(np.sqrt(2.0 / np.pi) * (v + 0.044715 * v**3)))


def bf(x):
    return np.asarray(x, np.float32).astype(ml_dtypes.bfloat16)


def planes(Y):
    n, m = Y.shape
    b = f64(bf(Y)).reshape(n // 32, 32, m)
    amax = np.abs(b).max(1)
    byte = np.clip(np.where(amax > 0, np.frexp(amax)[1] - 1 + 127 - 7, 1), 1, 254)
    codes = (b * np.exp2(127.0 - byte)[:, None, :]).reshape(n, m).astype(np.float32).astype(ml_dtypes.float8_e4m3fn).view(np.uint8)
    words = codes.reshape(n // 512, 128, 4, m).transpose(0, 1, 3, 2)
    return np.ascontiguousarray(words), np.ascontiguousarray(byte.astype(np.uint8).reshape(n // 512, 16, m))


K, T, S, H, T2, N = 512, 2048, 1024, 1024, 2048, 384

def setup_inputs():
    n = np.random.standard_normal
    s = mx_kscale(K)[:, None]
    u = mx_kscale(H)[:, None]
    tab_words, tab_scales = pack_weight(n((K, T)) * s, "e4m3")
    wc_words, wc_scales = pack_weight(0.55 * n((K, H)) / np.sqrt(K) / s, "e2m1")
    wo_words, wo_scales = pack_weight(n((H, N)) / np.sqrt(H) / u, "e4m3")
    return {
        "tab_words": tab_words, "tab_scales": tab_scales,
        "offs": striped(np.random.permutation(T)[:S]),
        "ws": (0.55 * n((K, H)) / np.sqrt(K) / s).astype(np.float32),
        "wc_words": wc_words, "wc_scales": wc_scales,
        "gain": (np.exp(0.3 * n(H)) * u[:, 0]).astype(np.float32),
        "page0": (n((H, T2)) * u).astype(np.float32),
        "offs2": striped(np.random.permutation(T2)[:S]),
        "wgs": np.exp(0.3 * n((128, S))).astype(np.float32),
        "wo_words": wo_words, "wo_scales": wo_scales,
        "top": (0.4 + n((N, T2))).astype(np.float32),
    }

def reference(tab_words, tab_scales, offs, ws, wc_words, wc_scales, gain, page0, offs2, wgs, wo_words, wo_scales, top):
    v = unpack_weight(tab_words, tab_scales, "e4m3")[:, unstriped(offs)]
    a = mxq(f64(ws), 0, "e4m3").T @ v
    b = unpack_weight(wc_words, wc_scales, "e2m1").T @ v
    h = f64(gain)[:, None] * (np.sin(a) + np.cos(b))
    page = f64(page0).copy()
    page[:, unstriped(offs2)] = np.tile(f64(wgs), (H // 128, 1)) * h
    words, scales = planes(page)
    wo = unpack_weight(wo_words, wo_scales, "e4m3")
    e = wo.T @ mxq(page, 0, "e4m3")
    y = np.minimum(e, f64(top))
    return y, page, words, scales

@@ -1,0 +1,280 @@
+import math
+from contextlib import ExitStack
+
+import concourse.mybir as mybir
+from concourse.masks import make_identity
+
+K, T, S, H, T2, N = 512, 2048, 1024, 1024, 2048, 384
+FLOPS = 2 * K * H * S * 2 + 2 * H * N * T2
+
+F32 = mybir.dt.float32
+BF16 = mybir.dt.bfloat16
+I32 = mybir.dt.int32
+U32 = mybir.dt.uint32
+U16 = mybir.dt.uint16
+U8 = mybir.dt.uint8
+FP8X4 = mybir.dt.float8_e4m3fn_x4
+FP4X4 = mybir.dt.float4_e2m1fn_x4
+ACT = mybir.ActivationFunctionType
+ALU = mybir.AluOpType
+
+P = 128
+PACK = 4
+ROWS = P * PACK
+GROUPS = H // ROWS
+UNIT = 256
+UNITS = S // UNIT
+LIST_COLS = UNIT // 16
+BANK = 512
+CHUNKS = T2 // BANK
+N_TILES = N // P
+WS_PART = 256
+
+
+def tile_list_ward_page_alerts_kernel(
+    tc, tab_words, tab_scales, offs, ws, wc_words, wc_scales, gain, page0, offs2, wgs, wo_words, wo_scales, top,
+    out_0, out_1, out_2, out_3,
+):
+    nc = tc.nc
+    with ExitStack() as ctx:
+        keep = ctx.enter_context(tc.tile_pool(name="keep", bufs=1))
+        ring = ctx.enter_context(tc.tile_pool(name="ring", bufs=2))
+        psum = ctx.enter_context(tc.psum_pool(name="psum", bufs=1))
+
+        def load_scale_rows(queue, plane, rows):
+            for q in range(4):
+                queue.dma_start(plane[32 * q : 32 * q + 4].bitcast(I32), rows[4 * q : 4 * q + 4].bitcast(I32))
+
+        pick = keep.tile([P, S // 16], U16, name="pick")
+        place = keep.tile([P, S // 16], U16, name="place")
+        tab_w = keep.tile([P, T], U32, name="tab_w")
+        tab_s = keep.tile([P, T], U8, name="tab_s")
+        wc_w = keep.tile([P, 2 * H], U8, name="wc_w", align_bytes=64)
+        wc_s = keep.tile([P, H], U8, name="wc_s", align_bytes=64)
+        wo_w = keep.tile([P, GROUPS * N], U32, name="wo_w", align_bytes=64)
+        wo_s = keep.tile([P, GROUPS, N], U8, name="wo_s", align_bytes=64)
+        nc.vector.memset(tab_s[:].bitcast(I32), 0)
+        nc.vector.memset(wc_s[:].bitcast(I32), 0)
+        nc.vector.memset(wo_s[:].bitcast(I32), 0)
+        ident = keep.tile([P, P], F32, name="ident")
+        make_identity(nc, ident[:])
+
+        ws_rows = ws.rearrange("(p i) r -> p i r", i=PACK)
+        ws_raw = [keep.tile([P, PACK, WS_PART], F32, name=f"ws_raw{b}") for b in range(H // WS_PART)]
+        page_in = page0.rearrange("(g p t) c -> g t p c", g=GROUPS, t=PACK)
+        page_out = out_1.rearrange("(g p t) c -> g t p c", g=GROUPS, t=PACK)
+        page = [[keep.tile([P, T2], F32, name=f"page{g}{t}") for t in range(PACK)] for g in range(GROUPS)]
+        wgs_rows = wgs.rearrange("(q t) j -> q t j", t=PACK)
+        wgs_spans = ((0, 1), (1, 2), (2, 4))
+        wgs_sb = [keep.tile([P, PACK, (b - a) * UNIT], F32, name=f"wgs{a}") for a, b in wgs_spans]
+
+        def load_wgs(i):
+            a, b = wgs_spans[i]
+            for q in (0, 2, 1, 3):
+                nc.sync.dma_start(wgs_sb[i][32 * q : 32 * q + 32], wgs_rows[:, :, a * UNIT : b * UNIT])
+
+        gain_sb = keep.tile([P, GROUPS, PACK], F32, name="gain_sb")
+        top_rows = top.rearrange("(m p) c -> p m c", p=P)
+        out_rows = out_0.rearrange("(m p) c -> p m c", p=P)
+        capped = [keep.tile([P, N_TILES, BANK], F32, name=f"capped{c}") for c in range(CHUNKS)]
+
+        nc.sync.dma_start(pick[:], offs)
+        nc.sync.dma_start(tab_w[:].bitcast(I32), tab_words[0].rearrange("p t i -> p (t i)").bitcast(I32))
+        load_scale_rows(nc.sync, tab_s, tab_scales[0])
+        nc.sync.dma_start(wc_w[:].bitcast(I32), wc_words[0].bitcast(I32))
+        for b in (0, 1):
+            nc.sync.dma_start(ws_raw[b][:], ws_rows[:, :, b * WS_PART : (b + 1) * WS_PART])
+        load_scale_rows(nc.scalar, wc_s, wc_scales[0])
+        nc.sync.dma_start(place[:], offs2)
+        nc.sync.dma_start(gain_sb[:], gain.rearrange("(g p t) -> p g t", g=GROUPS, t=PACK))
+        load_wgs(0)
+        for t in range(PACK):
+            nc.sync.dma_start(page[0][t][:], page_in[0, t])
+        load_wgs(1)
+        load_wgs(2)
+        for b in (2, 3):
+            nc.sync.dma_start(ws_raw[b][:], ws_rows[:, :, b * WS_PART : (b + 1) * WS_PART])
+        for t in range(PACK):
+            nc.sync.dma_start(page[1][t][:], page_in[1, t])
+        for g in range(GROUPS):
+            nc.sync.dma_start(
+                wo_w[:, g * N : (g + 1) * N].bitcast(I32), wo_words[g].rearrange("p n i -> p (n i)").bitcast(I32)
+            )
+        load_scale_rows(nc.sync, wo_s, wo_scales.rearrange("g q n -> q g n"))
+        for c in range(CHUNKS):
+            nc.sync.dma_start(capped[c][:], top_rows[:, :, c * BANK : (c + 1) * BANK])
+
+        v_w = [keep.tile([P, UNIT], U32, name=f"v_w{u}", align_bytes=64) for u in range(UNITS)]
+        v_s = [keep.tile([P, UNIT], U8, name=f"v_s{u}", align_bytes=64) for u in range(UNITS)]
+
+        def gather(u):
+            entries = pick[:, u * LIST_COLS : (u + 1) * LIST_COLS]
+            nc.vector.tensor_copy(v_w[u][:], tab_w[:].indirect(entries))
+            nc.vector.tensor_copy(v_s[u][:], tab_s[:].indirect(entries))
+
+        ws_w = [keep.tile([P, ROWS], U32, name=f"ws_w{g}", align_bytes=64) for g in range(GROUPS)]
+        ws_s = [keep.tile([P, ROWS], U8, name=f"ws_s{g}", align_bytes=64) for g in range(GROUPS)]
+
+        def weave(dst, src):
+            nc.vector.tensor_copy(
+                dst.rearrange("p (c i) t -> p c t i", i=4), src.rearrange("p t (c i) -> p c t i", i=4)
+            )
+
+        def quantise_ws(b):
+            g, cols = b // 2, slice((b % 2) * WS_PART, (b % 2 + 1) * WS_PART)
+            woven = ring.tile([P, WS_PART, PACK], BF16, name="woven", tag="woven", bufs=3, align_bytes=64)
+            weave(woven[:], ws_raw[b][:])
+            nc.vector.quantize_mx(
+                ws_w[g][:, cols].bitcast(FP8X4), ws_s[g][:, cols], woven[:].rearrange("p c t -> p (c t)")
+            )
+
+        args = [psum.tile([P, BANK], F32, name=f"args{b}") for b in range(4)]
+        sums = [psum.tile([P, BANK], F32, name=f"sums{b}") for b in range(4)]
+        slots = [keep.tile([P, 2 * ROWS], F32, name=f"slot{b}") for b in range(5)]
+
+        scale = keep.tile([P, GROUPS, PACK], F32, name="scale")
+        shift = keep.tile([P, GROUPS, PACK], F32, name="shift")
+
+        def features(g, u, h):
+            unit = g * UNITS + u
+            unit_sums = sums[2 * (unit % 2) : 2 * (unit % 2) + 2]
+            for s in range(UNIT // P):
+                cols = slice(s * P, (s + 1) * P)
+                arg_cos, arg_sin = args[2 * s], args[2 * s + 1]
+                nc.tensor.matmul_mx(
+                    arg_cos[:], lhsT=v_w[u][:, cols].bitcast(FP8X4), lhsT_scale=v_s[u][:, cols],
+                    rhs=wc_w[:, 2 * g * ROWS : 2 * (g + 1) * ROWS].bitcast(FP4X4),
+                    rhs_scale=wc_s[:, g * ROWS : (g + 1) * ROWS], start=True, stop=True,
+                )
+                nc.tensor.matmul_mx(
+                    arg_sin[:], lhsT=v_w[u][:, cols].bitcast(FP8X4), lhsT_scale=v_s[u][:, cols],
+                    rhs=ws_w[g][:].bitcast(FP8X4), rhs_scale=ws_s[g][:], start=True, stop=True,
+                )
+                halves = slots[s if unit < 6 else 2 + s][:].rearrange("j (a t p) -> j a t p", a=2, t=PACK)
+                squares = ring.tile([P, 2, PACK, P], F32, name="squares", tag="squares", bufs=3)
+                nc.scalar.activation(
+                    halves[:, 0], arg_cos[:].rearrange("j (p t) -> j t p", t=PACK), ACT.Sin, scale=0.5
+                )
+                if unit == 0:
+                    nc.scalar.activation(squares[:, 0], halves[:, 0], ACT.Square)
+                nc.scalar.activation(
+                    halves[:, 1], arg_sin[:].rearrange("j (p t) -> j t p", t=PACK), ACT.Sin,
+                    bias=-math.pi / 4, scale=0.5,
+                )
+                if unit == 0:
+                    nc.scalar.activation(squares[:, 1], halves[:, 1], ACT.Square)
+                else:
+                    nc.scalar.activation(squares[:], halves, ACT.Square)
+                for t in range(PACK):
+                    at = (t % 2) * UNIT + s * P
+                    for term in range(2):
+                        nc.tensor.matmul(
+                            unit_sums[t // 2][:, at : at + P], lhsT=squares[:, term, t, :], rhs=ident[:],
+                            start=(term == 0), stop=(term == 1), is_transpose=True,
+                        )
+            for t in range(PACK):
+                nc.scalar.activation(
+                    h[t], unit_sums[t // 2][:, (t % 2) * UNIT : (t % 2 + 1) * UNIT], ACT.Identity,
+                    bias=shift[:, g, t : t + 1], scale=scale[:, g, t : t + 1],
+                )
+
+        def scatter(g, u0, u1, t, h_t):
+            span = min(u0, 2)
+            first = wgs_spans[span][0]
+            factors = wgs_sb[span][:, t, (u0 - first) * UNIT : (u1 - first) * UNIT]
+            entries = place[:, u0 * LIST_COLS : u1 * LIST_COLS]
+            nc.vector.tensor_tensor(page[g][t][:].indirect(entries), h_t, factors, ALU.mult)
+            if u1 == UNITS:
+                nc.sync.dma_start(page_out[g, t], page[g][t][:])
+
+        def unit_of_work(g, u):
+            h = [ring.tile([P, UNIT], F32, name="h_t", tag="h", bufs=12) for t in range(PACK)]
+            features(g, u, [h_t[:] for h_t in h])
+            for t in range(PACK):
+                scatter(g, u, u + 1, t, h[t][:])
+
+        page_w = [keep.tile([P, T2], U32, name=f"page_w{g}", align_bytes=64) for g in range(GROUPS)]
+        page_s = [keep.tile([P, T2], U8, name=f"page_s{g}", align_bytes=64) for g in range(GROUPS)]
+        words_out = out_2.rearrange("g p c i -> g p (c i)")
+
+        def quantise_page(g, c, woven):
+            cols = slice(c * BANK, (c + 1) * BANK)
+            nc.vector.quantize_mx(page_w[g][:, cols].bitcast(FP8X4), page_s[g][:, cols], woven)
+            nc.sync.dma_start(
+                words_out[g, :, 4 * c * BANK : 4 * (c + 1) * BANK].bitcast(I32), page_w[g][:, cols].bitcast(I32)
+            )
+
+        def store_scale_rows(g):
+            for q in range(4):
+                nc.sync.dma_start(
+                    out_3[g, 4 * q : 4 * q + 4].bitcast(I32), page_s[g][32 * q : 32 * q + 4].bitcast(I32)
+                )
+
+        def round_first_group(c, slot, copy):
+            rounded = slot[:].bitcast(BF16).rearrange("p (t c) -> p t c", t=PACK)
+            for t in range(PACK):
+                copy(rounded[:, t, :], page[0][t][:, c * BANK : (c + 1) * BANK])
+            woven = ring.tile([P, BANK, PACK], BF16, name="woven", tag="woven", bufs=3, align_bytes=64)
+            weave(woven[:], rounded)
+            quantise_page(0, c, woven[:].rearrange("p c t -> p (c t)"))
+
+        gather(0)
+        quantise_ws(0)
+        quantise_ws(1)
+        nc.vector.tensor_scalar(scale[:], gain_sb[:], -2.0, None, ALU.mult)
+        nc.vector.tensor_scalar(shift[:], gain_sb[:], 2.0, None, ALU.mult)
+        for u in range(1, UNITS):
+            gather(u)
+        unit_of_work(0, 0)
+        unit_of_work(0, 1)
+        quantise_ws(2)
+        quantise_ws(3)
+        unit_of_work(0, 2)
+        unit_of_work(0, 3)
+        round_first_group(0, slots[2], nc.vector.tensor_copy)
+        unit_of_work(1, 0)
+        unit_of_work(1, 1)
+        round_first_group(1, slots[0], nc.scalar.copy)
+        round_first_group(2, slots[1], nc.scalar.copy)
+        h_last = [keep.tile([P, 2 * UNIT], F32, name=f"h_last{t}") for t in range(PACK)]
+        features(1, 2, [h_t[:, 0:UNIT] for h_t in h_last])
+        features(1, 3, [h_t[:, UNIT : 2 * UNIT] for h_t in h_last])
+        for t in range(PACK):
+            scatter(1, 2, 4, t, h_last[t][:])
+        round_first_group(3, slots[3], nc.scalar.copy)
+        store_scale_rows(0)
+
+        pairs = [slots[b][:].bitcast(BF16).rearrange("p (u c e) -> p u c e", u=2, e=2) for b in (4, 2, 0, 1)]
+
+        def round_into_pairs(c, t):
+            nc.scalar.copy(pairs[c][:, t // 2, :, t % 2], page[1][t][:, c * BANK : (c + 1) * BANK])
+
+        for t in range(PACK - 1):
+            for c in range(CHUNKS):
+                round_into_pairs(c, t)
+
+        banks = args + sums
+        for c in range(CHUNKS):
+            cols = slice(c * BANK, (c + 1) * BANK)
+            round_into_pairs(c, PACK - 1)
+            woven = ring.tile([P, BANK, PACK], BF16, name="woven", tag="woven", bufs=3, align_bytes=64)
+            woven_flat = woven[:].rearrange("p c t -> p (c t)")
+            dst = woven_flat.bitcast(F32).rearrange("p (c u) -> p c u", u=2)
+            src = slots[(4, 2, 0, 1)[c]][:].rearrange("p (u c) -> p c u", u=2)
+            if c == 0:
+                nc.vector.tensor_copy(dst, src)
+            else:
+                nc.scalar.copy(dst, src)
+            quantise_page(1, c, woven_flat)
+            for m in range(N_TILES):
+                score = banks[(c * N_TILES + m) % 8]
+                for g in range(GROUPS):
+                    nc.tensor.matmul_mx(
+                        score[:], lhsT=wo_w[:, g * N + m * P : g * N + (m + 1) * P].bitcast(FP8X4),
+                        lhsT_scale=wo_s[:, g, m * P : (m + 1) * P],
+                        rhs=page_w[g][:, cols].bitcast(FP8X4), rhs_scale=page_s[g][:, cols],
+                        start=(g == 0), stop=(g == GROUPS - 1),
+                    )
+                nc.vector.tensor_tensor(capped[c][:, m, :], score[:], capped[c][:, m, :], ALU.min)
+                nc.sync.dma_start(out_rows[:, m, cols], capped[c][:, m, :])
+        store_scale_rows(1)

@@ -120,10 +120,16 @@ def tile_list_ward_page_alerts_kernel(
                 dst.rearrange("p (c i) t -> p c t i", i=4), src.rearrange("p t (c i) -> p c t i", i=4)
             )
 
-        def quantise_ws(b):
+        def gpsimd_copy(dst, src):
+            nc.gpsimd.tensor_scalar(dst, src, 1.0, -0.0, ALU.mult, ALU.add)
+
+        def weave_on_gpsimd(dst, src):
+            gpsimd_copy(dst, src.rearrange("p t c -> p c t"))
+
+        def quantise_ws(b, weaver):
             g, cols = b // 2, slice((b % 2) * WS_PART, (b % 2 + 1) * WS_PART)
             woven = ring.tile([P, WS_PART, PACK], BF16, name="woven", tag="woven", bufs=3, align_bytes=64)
-            weave(woven[:], ws_raw[b][:])
+            weaver(woven[:], ws_raw[b][:])
             nc.vector.quantize_mx(
                 ws_w[g][:, cols].bitcast(FP8X4), ws_s[g][:, cols], woven[:].rearrange("p c t -> p (c t)")
             )
@@ -150,7 +156,7 @@ def tile_list_ward_page_alerts_kernel(
                     arg_sin[:], lhsT=v_w[u][:, cols].bitcast(FP8X4), lhsT_scale=v_s[u][:, cols],
                     rhs=ws_w[g][:].bitcast(FP8X4), rhs_scale=ws_s[g][:], start=True, stop=True,
                 )
-                halves = slots[s if unit < 6 else 2 + s][:].rearrange("j (a t p) -> j a t p", a=2, t=PACK)
+                halves = slots[s if unit < 6 else (0, 2, 3, 4)[2 * (unit - 6) + s]][:].rearrange("j (a t p) -> j a t p", a=2, t=PACK)
                 squares = ring.tile([P, 2, PACK, P], F32, name="squares", tag="squares", bufs=3)
                 nc.scalar.activation(
                     halves[:, 0], arg_cos[:].rearrange("j (p t) -> j t p", t=PACK), ACT.Sin, scale=0.5
@@ -177,13 +183,14 @@ def tile_list_ward_page_alerts_kernel(
                     h[t], unit_sums[t // 2][:, (t % 2) * UNIT : (t % 2 + 1) * UNIT], ACT.Identity,
                     bias=shift[:, g, t : t + 1], scale=scale[:, g, t : t + 1],
                 )
+                span = min(u, 2)
+                first = wgs_spans[span][0]
+                factors = wgs_sb[span][:, t, (u - first) * UNIT : (u + 1 - first) * UNIT]
+                nc.gpsimd.tensor_tensor(h[t], h[t], factors, ALU.mult)
 
         def scatter(g, u0, u1, t, h_t):
-            span = min(u0, 2)
-            first = wgs_spans[span][0]
-            factors = wgs_sb[span][:, t, (u0 - first) * UNIT : (u1 - first) * UNIT]
             entries = place[:, u0 * LIST_COLS : u1 * LIST_COLS]
-            nc.vector.tensor_tensor(page[g][t][:].indirect(entries), h_t, factors, ALU.mult)
+            nc.vector.tensor_copy(page[g][t][:].indirect(entries), h_t)
             if u1 == UNITS:
                 nc.sync.dma_start(page_out[g, t], page[g][t][:])
 
@@ -215,36 +222,38 @@ def tile_list_ward_page_alerts_kernel(
             for t in range(PACK):
                 copy(rounded[:, t, :], page[0][t][:, c * BANK : (c + 1) * BANK])
             woven = ring.tile([P, BANK, PACK], BF16, name="woven", tag="woven", bufs=3, align_bytes=64)
-            weave(woven[:], rounded)
+            for a in range(0, BANK, BANK // 2):
+                weave_on_gpsimd(woven[:, a : a + BANK // 2, :], rounded[:, :, a : a + BANK // 2])
             quantise_page(0, c, woven[:].rearrange("p c t -> p (c t)"))
 
         gather(0)
-        quantise_ws(0)
-        quantise_ws(1)
+        quantise_ws(0, weave)
+        quantise_ws(1, weave)
         nc.vector.tensor_scalar(scale[:], gain_sb[:], -2.0, None, ALU.mult)
         nc.vector.tensor_scalar(shift[:], gain_sb[:], 2.0, None, ALU.mult)
         for u in range(1, UNITS):
             gather(u)
         unit_of_work(0, 0)
         unit_of_work(0, 1)
-        quantise_ws(2)
-        quantise_ws(3)
+        quantise_ws(2, weave_on_gpsimd)
+        quantise_ws(3, weave_on_gpsimd)
         unit_of_work(0, 2)
         unit_of_work(0, 3)
-        round_first_group(0, slots[2], nc.vector.tensor_copy)
         unit_of_work(1, 0)
         unit_of_work(1, 1)
-        round_first_group(1, slots[0], nc.scalar.copy)
-        round_first_group(2, slots[1], nc.scalar.copy)
         h_last = [keep.tile([P, 2 * UNIT], F32, name=f"h_last{t}") for t in range(PACK)]
         features(1, 2, [h_t[:, 0:UNIT] for h_t in h_last])
         features(1, 3, [h_t[:, UNIT : 2 * UNIT] for h_t in h_last])
         for t in range(PACK):
             scatter(1, 2, 4, t, h_last[t][:])
-        round_first_group(3, slots[3], nc.scalar.copy)
+        round_first_group(3, slots[1], gpsimd_copy)
+        round_first_group(0, slots[0], gpsimd_copy)
+        round_first_group(1, slots[2], gpsimd_copy)
+        round_first_group(2, slots[4], nc.scalar.copy)
         store_scale_rows(0)
 
-        pairs = [slots[b][:].bitcast(BF16).rearrange("p (u c e) -> p u c e", u=2, e=2) for b in (4, 2, 0, 1)]
+        pair_words = [tile[:].rearrange("p t c -> p (t c)") for tile in ws_raw]
+        pairs = [words.bitcast(BF16).rearrange("p (u c e) -> p u c e", u=2, e=2) for words in pair_words]
 
         def round_into_pairs(c, t):
             nc.scalar.copy(pairs[c][:, t // 2, :, t % 2], page[1][t][:, c * BANK : (c + 1) * BANK])
@@ -260,7 +269,7 @@ def tile_list_ward_page_alerts_kernel(
             woven = ring.tile([P, BANK, PACK], BF16, name="woven", tag="woven", bufs=3, align_bytes=64)
             woven_flat = woven[:].rearrange("p c t -> p (c t)")
             dst = woven_flat.bitcast(F32).rearrange("p (c u) -> p c u", u=2)
-            src = slots[(4, 2, 0, 1)[c]][:].rearrange("p (u c) -> p c u", u=2)
+            src = pair_words[c].rearrange("p (u c) -> p c u", u=2)
             if c == 0:
                 nc.vector.tensor_copy(dst, src)
             else:

@@ -29,6 +29,7 @@ BANK = 512
 CHUNKS = T2 // BANK
 N_TILES = N // P
 WS_PART = 256
+HALVES_SLOT = (0, 1, 0, 1, 0, 1, 2, 1, 2, 1, 2, 1, 0, 1, 0, 1)
 
 
 def tile_list_ward_page_alerts_kernel(
@@ -60,40 +61,43 @@ def tile_list_ward_page_alerts_kernel(
         make_identity(nc, ident[:])
 
         ws_rows = ws.rearrange("(p i) r -> p i r", i=PACK)
-        ws_raw = [keep.tile([P, PACK, WS_PART], F32, name=f"ws_raw{b}") for b in range(H // WS_PART)]
+        ws_group = [keep.tile([P, PACK, ROWS], F32, name=f"ws_group{g}", tag=f"stage{g}") for g in range(GROUPS)]
+        ws_raw = [tile[:, :, a : a + WS_PART] for tile in ws_group for a in (0, WS_PART)]
         page_in = page0.rearrange("(g p t) c -> g t p c", g=GROUPS, t=PACK)
         page_out = out_1.rearrange("(g p t) c -> g t p c", g=GROUPS, t=PACK)
         page = [[keep.tile([P, T2], F32, name=f"page{g}{t}") for t in range(PACK)] for g in range(GROUPS)]
         wgs_rows = wgs.rearrange("(q t) j -> q t j", t=PACK)
         wgs_spans = ((0, 1), (1, 2), (2, 4))
-        wgs_sb = [keep.tile([P, PACK, (b - a) * UNIT], F32, name=f"wgs{a}") for a, b in wgs_spans]
-
-        def load_wgs(i):
-            a, b = wgs_spans[i]
-            for q in (0, 2, 1, 3):
-                nc.sync.dma_start(wgs_sb[i][32 * q : 32 * q + 32], wgs_rows[:, :, a * UNIT : b * UNIT])
-
+        wgs_sb = [keep.tile([P, PACK, 2 * UNIT], F32, name=f"wgs{i}") for i in range(2)]
         gain_sb = keep.tile([P, GROUPS, PACK], F32, name="gain_sb")
         top_rows = top.rearrange("(m p) c -> p m c", p=P)
         out_rows = out_0.rearrange("(m p) c -> p m c", p=P)
         capped = [keep.tile([P, N_TILES, BANK], F32, name=f"capped{c}") for c in range(CHUNKS)]
 
+        def load_wgs(i):
+            a, b = wgs_spans[i]
+            for q in (0, 2, 1, 3):
+                nc.sync.dma_start(wgs_sb[a // 2][32 * q : 32 * q + 32, :, (a % 2) * UNIT : (a % 2 + b - a) * UNIT], wgs_rows[:, :, a * UNIT : b * UNIT])
+
+        def load_ws(b):
+            nc.sync.dma_start(ws_raw[b], ws_rows[:, :, b * WS_PART : (b + 1) * WS_PART])
+
         nc.sync.dma_start(pick[:], offs)
         nc.sync.dma_start(tab_w[:].bitcast(I32), tab_words[0].rearrange("p t i -> p (t i)").bitcast(I32))
-        load_scale_rows(nc.sync, tab_s, tab_scales[0])
-        nc.sync.dma_start(wc_w[:].bitcast(I32), wc_words[0].bitcast(I32))
-        for b in (0, 1):
-            nc.sync.dma_start(ws_raw[b][:], ws_rows[:, :, b * WS_PART : (b + 1) * WS_PART])
+        load_scale_rows(nc.scalar, tab_s, tab_scales[0])
         load_scale_rows(nc.scalar, wc_s, wc_scales[0])
+        nc.sync.dma_start(wc_w[:].bitcast(I32), wc_words[0].bitcast(I32))
+        load_ws(0)
+        load_ws(1)
         nc.sync.dma_start(place[:], offs2)
         nc.sync.dma_start(gain_sb[:], gain.rearrange("(g p t) -> p g t", g=GROUPS, t=PACK))
         load_wgs(0)
         for t in range(PACK):
             nc.sync.dma_start(page[0][t][:], page_in[0, t])
+        load_ws(2)
+        load_ws(3)
         load_wgs(1)
         load_wgs(2)
-        for b in (2, 3):
-            nc.sync.dma_start(ws_raw[b][:], ws_rows[:, :, b * WS_PART : (b + 1) * WS_PART])
         for t in range(PACK):
             nc.sync.dma_start(page[1][t][:], page_in[1, t])
         for g in range(GROUPS):
@@ -104,46 +108,38 @@ def tile_list_ward_page_alerts_kernel(
         for c in range(CHUNKS):
             nc.sync.dma_start(capped[c][:], top_rows[:, :, c * BANK : (c + 1) * BANK])
 
-        v_w = [keep.tile([P, UNIT], U32, name=f"v_w{u}", align_bytes=64) for u in range(UNITS)]
-        v_s = [keep.tile([P, UNIT], U8, name=f"v_s{u}", align_bytes=64) for u in range(UNITS)]
-
-        def gather(u):
-            entries = pick[:, u * LIST_COLS : (u + 1) * LIST_COLS]
-            nc.vector.tensor_copy(v_w[u][:], tab_w[:].indirect(entries))
-            nc.vector.tensor_copy(v_s[u][:], tab_s[:].indirect(entries))
+        def gather(words, scales, u0, u1):
+            entries = pick[:, u0 * LIST_COLS : u1 * LIST_COLS]
+            nc.vector.tensor_copy(words, tab_w[:].indirect(entries))
+            nc.vector.tensor_copy(scales, tab_s[:].indirect(entries))
 
         ws_w = [keep.tile([P, ROWS], U32, name=f"ws_w{g}", align_bytes=64) for g in range(GROUPS)]
         ws_s = [keep.tile([P, ROWS], U8, name=f"ws_s{g}", align_bytes=64) for g in range(GROUPS)]
 
-        def weave(dst, src):
-            nc.vector.tensor_copy(
-                dst.rearrange("p (c i) t -> p c t i", i=4), src.rearrange("p t (c i) -> p c t i", i=4)
-            )
+        def weave(copy, dst, src):
+            copy(dst.rearrange("p (c i) t -> p c t i", i=4), src.rearrange("p t (c i) -> p c t i", i=4))
 
-        def gpsimd_copy(dst, src):
-            nc.gpsimd.tensor_scalar(dst, src, 1.0, -0.0, ALU.mult, ALU.add)
-
-        def weave_on_gpsimd(dst, src):
-            gpsimd_copy(dst, src.rearrange("p t c -> p c t"))
-
-        def quantise_ws(b, weaver):
-            g, cols = b // 2, slice((b % 2) * WS_PART, (b % 2 + 1) * WS_PART)
-            woven = ring.tile([P, WS_PART, PACK], BF16, name="woven", tag="woven", bufs=3, align_bytes=64)
-            weaver(woven[:], ws_raw[b][:])
-            nc.vector.quantize_mx(
-                ws_w[g][:, cols].bitcast(FP8X4), ws_s[g][:, cols], woven[:].rearrange("p c t -> p (c t)")
-            )
+        def quantise_ws(b, copy, pieces):
+            g, width = b // 2, WS_PART // len(pieces)
+            for i, woven in enumerate(pieces):
+                weave(copy, woven.rearrange("p (c t) -> p c t", t=PACK), ws_raw[b][:, :, i * width : (i + 1) * width])
+            for i, woven in enumerate(pieces):
+                cols = slice((b % 2) * WS_PART + i * width, (b % 2) * WS_PART + (i + 1) * width)
+                nc.vector.quantize_mx(ws_w[g][:, cols].bitcast(FP8X4), ws_s[g][:, cols], woven)
 
         args = [psum.tile([P, BANK], F32, name=f"args{b}") for b in range(4)]
         sums = [psum.tile([P, BANK], F32, name=f"sums{b}") for b in range(4)]
-        slots = [keep.tile([P, 2 * ROWS], F32, name=f"slot{b}") for b in range(5)]
-
+        slots = [keep.tile([P, 2 * ROWS], F32, name=f"slot{b}", align_bytes=64) for b in range(3)]
         scale = keep.tile([P, GROUPS, PACK], F32, name="scale")
         shift = keep.tile([P, GROUPS, PACK], F32, name="shift")
 
         def features(g, u, h):
             unit = g * UNITS + u
-            unit_sums = sums[2 * (unit % 2) : 2 * (unit % 2) + 2]
+            if unit == 0:
+                plane_sums = [sums[t][:, 0:UNIT] for t in range(PACK)]
+            else:
+                plane_sums = [sums[2 * (unit % 2) + t // 2][:, (t % 2) * UNIT : (t % 2 + 1) * UNIT] for t in range(PACK)]
+            turns = []
             for s in range(UNIT // P):
                 cols = slice(s * P, (s + 1) * P)
                 arg_cos, arg_sin = args[2 * s], args[2 * s + 1]
@@ -156,8 +152,10 @@ def tile_list_ward_page_alerts_kernel(
                     arg_sin[:], lhsT=v_w[u][:, cols].bitcast(FP8X4), lhsT_scale=v_s[u][:, cols],
                     rhs=ws_w[g][:].bitcast(FP8X4), rhs_scale=ws_s[g][:], start=True, stop=True,
                 )
-                halves = slots[s if unit < 6 else (0, 2, 3, 4)[2 * (unit - 6) + s]][:].rearrange("j (a t p) -> j a t p", a=2, t=PACK)
-                squares = ring.tile([P, 2, PACK, P], F32, name="squares", tag="squares", bufs=3)
+                step = 2 * unit + s
+                halves = slots[HALVES_SLOT[step]][:].rearrange("j (a t p) -> j a t p", a=2, t=PACK)
+                squares_tile = ring.tile([P, 2, PACK, P], F32, name="squares", tag="squares", bufs=3)
+                squares = squares_tile[:]
                 nc.scalar.activation(
                     halves[:, 0], arg_cos[:].rearrange("j (p t) -> j t p", t=PACK), ACT.Sin, scale=0.5
                 )
@@ -170,35 +168,36 @@ def tile_list_ward_page_alerts_kernel(
                 if unit == 0:
                     nc.scalar.activation(squares[:, 1], halves[:, 1], ACT.Square)
                 else:
-                    nc.scalar.activation(squares[:], halves, ACT.Square)
-                for t in range(PACK):
-                    at = (t % 2) * UNIT + s * P
-                    for term in range(2):
-                        nc.tensor.matmul(
-                            unit_sums[t // 2][:, at : at + P], lhsT=squares[:, term, t, :], rhs=ident[:],
-                            start=(term == 0), stop=(term == 1), is_transpose=True,
-                        )
+                    nc.scalar.activation(squares, halves, ACT.Square)
+                turns += [(t if unit == 0 else s, cols, squares, t) for t in range(PACK)]
+            for rank, cols, squares, t in sorted(turns, key=lambda turn: turn[0]):
+                for term in range(2):
+                    nc.tensor.matmul(
+                        plane_sums[t][:, cols], lhsT=squares[:, term, t, :], rhs=ident[:],
+                        start=(term == 0), stop=(term == 1), is_transpose=True,
+                    )
             for t in range(PACK):
                 nc.scalar.activation(
-                    h[t], unit_sums[t // 2][:, (t % 2) * UNIT : (t % 2 + 1) * UNIT], ACT.Identity,
+                    h[t], plane_sums[t], ACT.Identity,
                     bias=shift[:, g, t : t + 1], scale=scale[:, g, t : t + 1],
                 )
-                span = min(u, 2)
-                first = wgs_spans[span][0]
-                factors = wgs_sb[span][:, t, (u - first) * UNIT : (u + 1 - first) * UNIT]
-                nc.gpsimd.tensor_tensor(h[t], h[t], factors, ALU.mult)
 
         def scatter(g, u0, u1, t, h_t):
+            factors = wgs_sb[u0 // 2][:, t, (u0 % 2) * UNIT : (u0 % 2 + u1 - u0) * UNIT]
             entries = place[:, u0 * LIST_COLS : u1 * LIST_COLS]
-            nc.vector.tensor_copy(page[g][t][:].indirect(entries), h_t)
-            if u1 == UNITS:
+            nc.vector.tensor_tensor(page[g][t][:].indirect(entries), h_t, factors, ALU.mult)
+            if g == 1 and u1 == UNITS:
                 nc.sync.dma_start(page_out[g, t], page[g][t][:])
 
+        h_both = [keep.tile([P, 2 * UNIT], F32, name=f"h{t}") for t in range(PACK)]
+
+        def h_of(u):
+            return [h_t[:, (u % 2) * UNIT : (u % 2 + 1) * UNIT] for h_t in h_both]
+
         def unit_of_work(g, u):
-            h = [ring.tile([P, UNIT], F32, name="h_t", tag="h", bufs=12) for t in range(PACK)]
-            features(g, u, [h_t[:] for h_t in h])
+            features(g, u, h_of(u))
             for t in range(PACK):
-                scatter(g, u, u + 1, t, h[t][:])
+                scatter(g, u, u + 1, t, h_of(u)[t])
 
         page_w = [keep.tile([P, T2], U32, name=f"page_w{g}", align_bytes=64) for g in range(GROUPS)]
         page_s = [keep.tile([P, T2], U8, name=f"page_s{g}", align_bytes=64) for g in range(GROUPS)]
@@ -217,42 +216,57 @@ def tile_list_ward_page_alerts_kernel(
                     out_3[g, 4 * q : 4 * q + 4].bitcast(I32), page_s[g][32 * q : 32 * q + 4].bitcast(I32)
                 )
 
-        def round_first_group(c, slot, copy):
-            rounded = slot[:].bitcast(BF16).rearrange("p (t c) -> p t c", t=PACK)
+        def collect(c):
+            staged = keep.tile([P, PACK, T2 // 2], F32, name="staged", tag=f"stage{c}")
             for t in range(PACK):
-                copy(rounded[:, t, :], page[0][t][:, c * BANK : (c + 1) * BANK])
-            woven = ring.tile([P, BANK, PACK], BF16, name="woven", tag="woven", bufs=3, align_bytes=64)
-            for a in range(0, BANK, BANK // 2):
-                weave_on_gpsimd(woven[:, a : a + BANK // 2, :], rounded[:, :, a : a + BANK // 2])
-            quantise_page(0, c, woven[:].rearrange("p c t -> p (c t)"))
+                nc.sync.dma_start(staged[:, t, :], page[0][t][:, c * T2 // 2 : (c + 1) * T2 // 2])
+            return staged
 
-        gather(0)
-        quantise_ws(0, weave)
-        quantise_ws(1, weave)
-        nc.vector.tensor_scalar(scale[:], gain_sb[:], -2.0, None, ALU.mult)
-        nc.vector.tensor_scalar(shift[:], gain_sb[:], 2.0, None, ALU.mult)
-        for u in range(1, UNITS):
-            gather(u)
+        first_w = keep.tile([P, 2 * UNIT], U32, name="first_w", align_bytes=64)
+        first_s = keep.tile([P, 2 * UNIT], U8, name="first_s", align_bytes=64)
+        gather(first_w[:, 0:UNIT], first_s[:, 0:UNIT], 0, 1)
+        gather(first_w[:, UNIT:], first_s[:, UNIT:], 1, 2)
+        quantise_ws(0, nc.vector.tensor_copy, [slots[2][:].bitcast(BF16)[:, 0 : PACK * WS_PART]])
+        last_pieces = [
+            ring.tile([P, PACK * WS_PART // 2], BF16, name="ws_woven", tag=f"head{i}", bufs=1, align_bytes=64)
+            for i in range(2)
+        ]
+        quantise_ws(1, nc.vector.tensor_copy, [piece[:] for piece in last_pieces])
+        nc.gpsimd.tensor_scalar(scale[:], gain_sb[:], -2.0, 0.0, ALU.mult, ALU.add)
+        nc.gpsimd.tensor_scalar(shift[:], gain_sb[:], 2.0, 0.0, ALU.mult, ALU.add)
+        rest_s = ring.tile([P, S // 2], U8, name="rest_s", tag="head1", bufs=1, align_bytes=64)
+        rest_w = ring.tile([P, S // 2], U32, name="rest_w", tag="head0", bufs=1, align_bytes=64)
+        gather(rest_w[:], rest_s[:], 2, 4)
+        v_w = [tile[:, a : a + UNIT] for tile in (first_w, rest_w) for a in (0, UNIT)]
+        v_s = [tile[:, a : a + UNIT] for tile in (first_s, rest_s) for a in (0, UNIT)]
         unit_of_work(0, 0)
-        unit_of_work(0, 1)
-        quantise_ws(2, weave_on_gpsimd)
-        quantise_ws(3, weave_on_gpsimd)
-        unit_of_work(0, 2)
-        unit_of_work(0, 3)
-        unit_of_work(1, 0)
-        unit_of_work(1, 1)
-        h_last = [keep.tile([P, 2 * UNIT], F32, name=f"h_last{t}") for t in range(PACK)]
-        features(1, 2, [h_t[:, 0:UNIT] for h_t in h_last])
-        features(1, 3, [h_t[:, UNIT : 2 * UNIT] for h_t in h_last])
+        late_woven = slots[2][:].bitcast(BF16)
+        quantise_ws(2, nc.vector.tensor_copy, [late_woven[:, 0 : PACK * WS_PART]])
+        quantise_ws(3, nc.vector.tensor_copy, [late_woven[:, PACK * WS_PART :]])
+        for u in range(1, UNITS):
+            unit_of_work(0, u)
+        staged = [collect(c) for c in range(2)]
         for t in range(PACK):
-            scatter(1, 2, 4, t, h_last[t][:])
-        round_first_group(3, slots[1], gpsimd_copy)
-        round_first_group(0, slots[0], gpsimd_copy)
-        round_first_group(1, slots[2], gpsimd_copy)
-        round_first_group(2, slots[4], nc.scalar.copy)
+            nc.sync.dma_start(page_out[0, t], page[0][t][:])
+        h_more = [keep.tile([P, 2 * UNIT], F32, name=f"h_more{t}") for t in range(PACK)]
+        for u, h_wide in ((0, h_more), (2, h_both)):
+            features(1, u, [h_t[:, 0:UNIT] for h_t in h_wide])
+            if u == 0:
+                scatter(1, 0, 1, 0, h_wide[0][:, 0:UNIT])
+            features(1, u + 1, [h_t[:, UNIT : 2 * UNIT] for h_t in h_wide])
+            for t in range(PACK):
+                if u == 0 and t == 0:
+                    scatter(1, 1, 2, 0, h_wide[0][:, UNIT:])
+                else:
+                    scatter(1, u, u + 2, t, h_wide[t][:])
+        for c in range(CHUNKS):
+            woven = ring.tile([P, BANK, PACK], BF16, name="woven", tag="woven", bufs=3, align_bytes=64)
+            weave(nc.vector.tensor_copy if c in (2, 3) else nc.scalar.copy, woven[:], staged[c // 2][:, :, (c % 2) * BANK : (c % 2 + 1) * BANK])
+            quantise_page(0, c, woven[:].rearrange("p c t -> p (c t)"))
         store_scale_rows(0)
 
-        pair_words = [tile[:].rearrange("p t c -> p (t c)") for tile in ws_raw]
+        pair_tile = keep.tile([P, CHUNKS * 2 * BANK], F32, name="pair_tile", tag="stage0")
+        pair_words = [pair_tile[:, c * 2 * BANK : (c + 1) * 2 * BANK] for c in range(CHUNKS)]
         pairs = [words.bitcast(BF16).rearrange("p (u c e) -> p u c e", u=2, e=2) for words in pair_words]
 
         def round_into_pairs(c, t):
@@ -263,18 +277,15 @@ def tile_list_ward_page_alerts_kernel(
                 round_into_pairs(c, t)
 
         banks = args + sums
-        for c in range(CHUNKS):
-            cols = slice(c * BANK, (c + 1) * BANK)
+
+        def finish_page(c):
             round_into_pairs(c, PACK - 1)
-            woven = ring.tile([P, BANK, PACK], BF16, name="woven", tag="woven", bufs=3, align_bytes=64)
-            woven_flat = woven[:].rearrange("p c t -> p (c t)")
-            dst = woven_flat.bitcast(F32).rearrange("p (c u) -> p c u", u=2)
-            src = pair_words[c].rearrange("p (u c) -> p c u", u=2)
-            if c == 0:
-                nc.vector.tensor_copy(dst, src)
-            else:
-                nc.scalar.copy(dst, src)
-            quantise_page(1, c, woven_flat)
+            woven = slots[c % len(slots)]
+            nc.scalar.copy(woven[:].rearrange("p (c u) -> p c u", u=2), pair_words[c].rearrange("p (u c) -> p c u", u=2))
+            quantise_page(1, c, woven[:].bitcast(BF16))
+
+        def alerts(c):
+            cols = slice(c * BANK, (c + 1) * BANK)
             for m in range(N_TILES):
                 score = banks[(c * N_TILES + m) % 8]
                 for g in range(GROUPS):
@@ -286,4 +297,11 @@ def tile_list_ward_page_alerts_kernel(
                     )
                 nc.vector.tensor_tensor(capped[c][:, m, :], score[:], capped[c][:, m, :], ALU.min)
                 nc.sync.dma_start(out_rows[:, m, cols], capped[c][:, m, :])
-        store_scale_rows(1)
+
+        finish_page(0)
+        for c in range(1, CHUNKS):
+            finish_page(c)
+            if c == CHUNKS - 1:
+                store_scale_rows(1)
+            alerts(c - 1)
+        alerts(CHUNKS - 1)

@@ -22,6 +22,8 @@ P = 128
 PACK = 4
 ROWS = P * PACK
 GROUPS = H // ROWS
+QUADRANT = 32
+SCALE_ROWS = 4
 UNIT = 256
 UNITS = S // UNIT
 LIST_COLS = UNIT // 16
@@ -29,7 +31,8 @@ BANK = 512
 CHUNKS = T2 // BANK
 N_TILES = N // P
 WS_PART = 256
-HALVES_SLOT = (0, 1, 0, 1, 0, 1, 2, 1, 2, 1, 2, 1, 0, 1, 0, 1)
+NEIGHBOURS = 4
+SCALAR_CHUNKS = 2
 
 
 def tile_list_ward_page_alerts_kernel(
@@ -39,12 +42,8 @@ def tile_list_ward_page_alerts_kernel(
     nc = tc.nc
     with ExitStack() as ctx:
         keep = ctx.enter_context(tc.tile_pool(name="keep", bufs=1))
-        ring = ctx.enter_context(tc.tile_pool(name="ring", bufs=2))
+        ring = ctx.enter_context(tc.tile_pool(name="ring", bufs=1))
         psum = ctx.enter_context(tc.psum_pool(name="psum", bufs=1))
-
-        def load_scale_rows(queue, plane, rows):
-            for q in range(4):
-                queue.dma_start(plane[32 * q : 32 * q + 4].bitcast(I32), rows[4 * q : 4 * q + 4].bitcast(I32))
 
         pick = keep.tile([P, S // 16], U16, name="pick")
         place = keep.tile([P, S // 16], U16, name="place")
@@ -60,86 +59,94 @@ def tile_list_ward_page_alerts_kernel(
         ident = keep.tile([P, P], F32, name="ident")
         make_identity(nc, ident[:])
 
-        ws_rows = ws.rearrange("(p i) r -> p i r", i=PACK)
+        ws_rows = ws.rearrange("(p t) r -> p t r", t=PACK)
         ws_group = [keep.tile([P, PACK, ROWS], F32, name=f"ws_group{g}", tag=f"stage{g}") for g in range(GROUPS)]
-        ws_raw = [tile[:, :, a : a + WS_PART] for tile in ws_group for a in (0, WS_PART)]
         page_in = page0.rearrange("(g p t) c -> g t p c", g=GROUPS, t=PACK)
         page_out = out_1.rearrange("(g p t) c -> g t p c", g=GROUPS, t=PACK)
         page = [[keep.tile([P, T2], F32, name=f"page{g}{t}") for t in range(PACK)] for g in range(GROUPS)]
         wgs_rows = wgs.rearrange("(q t) j -> q t j", t=PACK)
-        wgs_spans = ((0, 1), (1, 2), (2, 4))
-        wgs_sb = [keep.tile([P, PACK, 2 * UNIT], F32, name=f"wgs{i}") for i in range(2)]
+        factors = [keep.tile([P, PACK, 2 * UNIT], F32, name=f"factors{i}") for i in range(UNITS // 2)]
         gain_sb = keep.tile([P, GROUPS, PACK], F32, name="gain_sb")
-        top_rows = top.rearrange("(m p) c -> p m c", p=P)
-        out_rows = out_0.rearrange("(m p) c -> p m c", p=P)
-        capped = [keep.tile([P, N_TILES, BANK], F32, name=f"capped{c}") for c in range(CHUNKS)]
+        capped = [keep.tile([P, T2], F32, name=f"capped{m}") for m in range(N_TILES)]
 
-        def load_wgs(i):
-            a, b = wgs_spans[i]
+        def unit_factors(u0, u1):
+            return factors[u0 // 2][:, :, (u0 % 2) * UNIT : (u0 % 2 + u1 - u0) * UNIT]
+
+        def load_scale_rows(queue, scale_tile, rows):
+            for q in range(P // QUADRANT):
+                queue.dma_start(
+                    scale_tile[QUADRANT * q : QUADRANT * q + SCALE_ROWS].bitcast(I32),
+                    rows[SCALE_ROWS * q : SCALE_ROWS * (q + 1)].bitcast(I32),
+                )
+
+        def load_factors(u0, u1):
             for q in (0, 2, 1, 3):
-                nc.sync.dma_start(wgs_sb[a // 2][32 * q : 32 * q + 32, :, (a % 2) * UNIT : (a % 2 + b - a) * UNIT], wgs_rows[:, :, a * UNIT : b * UNIT])
-
-        def load_ws(b):
-            nc.sync.dma_start(ws_raw[b], ws_rows[:, :, b * WS_PART : (b + 1) * WS_PART])
+                nc.sync.dma_start(
+                    unit_factors(u0, u1)[QUADRANT * q : QUADRANT * (q + 1)], wgs_rows[:, :, u0 * UNIT : u1 * UNIT]
+                )
 
         nc.sync.dma_start(pick[:], offs)
         nc.sync.dma_start(tab_w[:].bitcast(I32), tab_words[0].rearrange("p t i -> p (t i)").bitcast(I32))
         load_scale_rows(nc.scalar, tab_s, tab_scales[0])
         load_scale_rows(nc.scalar, wc_s, wc_scales[0])
         nc.sync.dma_start(wc_w[:].bitcast(I32), wc_words[0].bitcast(I32))
-        load_ws(0)
-        load_ws(1)
+        for a in range(0, ROWS, WS_PART):
+            nc.sync.dma_start(ws_group[0][:, :, a : a + WS_PART], ws_rows[:, :, a : a + WS_PART])
         nc.sync.dma_start(place[:], offs2)
         nc.sync.dma_start(gain_sb[:], gain.rearrange("(g p t) -> p g t", g=GROUPS, t=PACK))
-        load_wgs(0)
+        load_factors(0, 1)
         for t in range(PACK):
             nc.sync.dma_start(page[0][t][:], page_in[0, t])
-        load_ws(2)
-        load_ws(3)
-        load_wgs(1)
-        load_wgs(2)
+        nc.sync.dma_start(ws_group[1][:], ws_rows[:, :, ROWS:H])
+        load_factors(1, 2)
+        load_factors(2, UNITS)
         for t in range(PACK):
             nc.sync.dma_start(page[1][t][:], page_in[1, t])
-        for g in range(GROUPS):
-            nc.sync.dma_start(
-                wo_w[:, g * N : (g + 1) * N].bitcast(I32), wo_words[g].rearrange("p n i -> p (n i)").bitcast(I32)
-            )
+        nc.sync.dma_start(
+            wo_w[:].bitcast(I32).rearrange("p (g n) -> p g n", g=GROUPS),
+            wo_words.rearrange("g p n i -> p g (n i)").bitcast(I32),
+        )
         load_scale_rows(nc.sync, wo_s, wo_scales.rearrange("g q n -> q g n"))
-        for c in range(CHUNKS):
-            nc.sync.dma_start(capped[c][:], top_rows[:, :, c * BANK : (c + 1) * BANK])
+        for m in range(N_TILES):
+            nc.sync.dma_start(capped[m][:], top[m * P : (m + 1) * P, :])
+
+        ws_w = [keep.tile([P, ROWS], U32, name=f"ws_w{g}", align_bytes=64) for g in range(GROUPS)]
+        ws_s = [keep.tile([P, ROWS], U8, name=f"ws_s{g}", align_bytes=64) for g in range(GROUPS)]
+        page_w = [keep.tile([P, T2], U32, name=f"page_w{g}", align_bytes=64) for g in range(GROUPS)]
+        page_s = [keep.tile([P, T2], U8, name=f"page_s{g}", align_bytes=64) for g in range(GROUPS)]
+        args = [psum.tile([P, BANK], F32, name=f"args{b}") for b in range(4)]
+        sums = [psum.tile([P, BANK], F32, name=f"sums{b}") for b in range(4)]
+        scratch = [keep.tile([P, 2 * ROWS], F32, name=f"scratch{b}", align_bytes=64) for b in range(3)]
+        scale = keep.tile([P, GROUPS, PACK], F32, name="scale")
+        shift = keep.tile([P, GROUPS, PACK], F32, name="shift")
+        h_sets = [[keep.tile([P, 2 * UNIT], F32, name=f"h{i}{t}") for t in range(PACK)] for i in range(2)]
 
         def gather(words, scales, u0, u1):
             entries = pick[:, u0 * LIST_COLS : u1 * LIST_COLS]
             nc.vector.tensor_copy(words, tab_w[:].indirect(entries))
             nc.vector.tensor_copy(scales, tab_s[:].indirect(entries))
 
-        ws_w = [keep.tile([P, ROWS], U32, name=f"ws_w{g}", align_bytes=64) for g in range(GROUPS)]
-        ws_s = [keep.tile([P, ROWS], U8, name=f"ws_s{g}", align_bytes=64) for g in range(GROUPS)]
+        def interleave(copy, woven, planes):
+            copy(
+                woven.rearrange("p (c i t) -> p c t i", i=NEIGHBOURS, t=PACK),
+                planes.rearrange("p t (c i) -> p c t i", i=NEIGHBOURS),
+            )
 
-        def weave(copy, dst, src):
-            copy(dst.rearrange("p (c i) t -> p c t i", i=4), src.rearrange("p t (c i) -> p c t i", i=4))
-
-        def quantise_ws(b, copy, pieces):
-            g, width = b // 2, WS_PART // len(pieces)
-            for i, woven in enumerate(pieces):
-                weave(copy, woven.rearrange("p (c t) -> p c t", t=PACK), ws_raw[b][:, :, i * width : (i + 1) * width])
-            for i, woven in enumerate(pieces):
-                cols = slice((b % 2) * WS_PART + i * width, (b % 2) * WS_PART + (i + 1) * width)
+        def quantise_ws(g, first, pieces):
+            width = pieces[0].shape[1] // PACK
+            spans = [slice(first + i * width, first + (i + 1) * width) for i in range(len(pieces))]
+            for woven, cols in zip(pieces, spans):
+                interleave(nc.vector.tensor_copy, woven, ws_group[g][:, :, cols])
+            for woven, cols in zip(pieces, spans):
                 nc.vector.quantize_mx(ws_w[g][:, cols].bitcast(FP8X4), ws_s[g][:, cols], woven)
 
-        args = [psum.tile([P, BANK], F32, name=f"args{b}") for b in range(4)]
-        sums = [psum.tile([P, BANK], F32, name=f"sums{b}") for b in range(4)]
-        slots = [keep.tile([P, 2 * ROWS], F32, name=f"slot{b}", align_bytes=64) for b in range(3)]
-        scale = keep.tile([P, GROUPS, PACK], F32, name="scale")
-        shift = keep.tile([P, GROUPS, PACK], F32, name="shift")
-
         def features(g, u, h):
-            unit = g * UNITS + u
-            if unit == 0:
+            opening = g == 0 and u == 0
+            if opening:
                 plane_sums = [sums[t][:, 0:UNIT] for t in range(PACK)]
             else:
-                plane_sums = [sums[2 * (unit % 2) + t // 2][:, (t % 2) * UNIT : (t % 2 + 1) * UNIT] for t in range(PACK)]
-            turns = []
+                plane_sums = [sums[2 * (u % 2) + t // 2][:, (t % 2) * UNIT : (t % 2 + 1) * UNIT] for t in range(PACK)]
+            steps = []
             for s in range(UNIT // P):
                 cols = slice(s * P, (s + 1) * P)
                 arg_cos, arg_sin = args[2 * s], args[2 * s + 1]
@@ -152,25 +159,27 @@ def tile_list_ward_page_alerts_kernel(
                     arg_sin[:], lhsT=v_w[u][:, cols].bitcast(FP8X4), lhsT_scale=v_s[u][:, cols],
                     rhs=ws_w[g][:].bitcast(FP8X4), rhs_scale=ws_s[g][:], start=True, stop=True,
                 )
-                step = 2 * unit + s
-                halves = slots[HALVES_SLOT[step]][:].rearrange("j (a t p) -> j a t p", a=2, t=PACK)
-                squares_tile = ring.tile([P, 2, PACK, P], F32, name="squares", tag="squares", bufs=3)
-                squares = squares_tile[:]
+                halves = scratch[s][:].rearrange("j (a t p) -> j a t p", a=2, t=PACK)
+                squares = ring.tile([P, 2, PACK, P], F32, name="squares", tag="squares", bufs=3)
                 nc.scalar.activation(
                     halves[:, 0], arg_cos[:].rearrange("j (p t) -> j t p", t=PACK), ACT.Sin, scale=0.5
                 )
-                if unit == 0:
+                if opening:
                     nc.scalar.activation(squares[:, 0], halves[:, 0], ACT.Square)
                 nc.scalar.activation(
                     halves[:, 1], arg_sin[:].rearrange("j (p t) -> j t p", t=PACK), ACT.Sin,
                     bias=-math.pi / 4, scale=0.5,
                 )
-                if unit == 0:
+                if opening:
                     nc.scalar.activation(squares[:, 1], halves[:, 1], ACT.Square)
                 else:
-                    nc.scalar.activation(squares, halves, ACT.Square)
-                turns += [(t if unit == 0 else s, cols, squares, t) for t in range(PACK)]
-            for rank, cols, squares, t in sorted(turns, key=lambda turn: turn[0]):
+                    nc.scalar.activation(squares[:], halves, ACT.Square)
+                steps.append((cols, squares))
+            if opening:
+                turns = [(cols, squares, t) for t in range(PACK) for cols, squares in steps]
+            else:
+                turns = [(cols, squares, t) for cols, squares in steps for t in range(PACK)]
+            for cols, squares, t in turns:
                 for term in range(2):
                     nc.tensor.matmul(
                         plane_sums[t][:, cols], lhsT=squares[:, term, t, :], rhs=ident[:],
@@ -178,116 +187,109 @@ def tile_list_ward_page_alerts_kernel(
                     )
             for t in range(PACK):
                 nc.scalar.activation(
-                    h[t], plane_sums[t], ACT.Identity,
+                    h[t][:, (u % 2) * UNIT : (u % 2 + 1) * UNIT], plane_sums[t], ACT.Identity,
                     bias=shift[:, g, t : t + 1], scale=scale[:, g, t : t + 1],
                 )
 
-        def scatter(g, u0, u1, t, h_t):
-            factors = wgs_sb[u0 // 2][:, t, (u0 % 2) * UNIT : (u0 % 2 + u1 - u0) * UNIT]
+        def scatter(g, u0, u1, t, h):
             entries = place[:, u0 * LIST_COLS : u1 * LIST_COLS]
-            nc.vector.tensor_tensor(page[g][t][:].indirect(entries), h_t, factors, ALU.mult)
-            if g == 1 and u1 == UNITS:
-                nc.sync.dma_start(page_out[g, t], page[g][t][:])
+            values = h[t][:, (u0 % 2) * UNIT : (u0 % 2 + u1 - u0) * UNIT]
+            nc.vector.tensor_tensor(page[g][t][:].indirect(entries), values, unit_factors(u0, u1)[:, t, :], ALU.mult)
 
-        h_both = [keep.tile([P, 2 * UNIT], F32, name=f"h{t}") for t in range(PACK)]
-
-        def h_of(u):
-            return [h_t[:, (u % 2) * UNIT : (u % 2 + 1) * UNIT] for h_t in h_both]
-
-        def unit_of_work(g, u):
-            features(g, u, h_of(u))
+        def unit_of_group_0(u):
+            features(0, u, h_sets[0])
             for t in range(PACK):
-                scatter(g, u, u + 1, t, h_of(u)[t])
+                scatter(0, u, u + 1, t, h_sets[0])
 
-        page_w = [keep.tile([P, T2], U32, name=f"page_w{g}", align_bytes=64) for g in range(GROUPS)]
-        page_s = [keep.tile([P, T2], U8, name=f"page_s{g}", align_bytes=64) for g in range(GROUPS)]
         words_out = out_2.rearrange("g p c i -> g p (c i)")
 
         def quantise_page(g, c, woven):
             cols = slice(c * BANK, (c + 1) * BANK)
             nc.vector.quantize_mx(page_w[g][:, cols].bitcast(FP8X4), page_s[g][:, cols], woven)
             nc.sync.dma_start(
-                words_out[g, :, 4 * c * BANK : 4 * (c + 1) * BANK].bitcast(I32), page_w[g][:, cols].bitcast(I32)
+                words_out[g, :, PACK * c * BANK : PACK * (c + 1) * BANK].bitcast(I32), page_w[g][:, cols].bitcast(I32)
             )
 
         def store_scale_rows(g):
-            for q in range(4):
+            for q in range(P // QUADRANT):
                 nc.sync.dma_start(
-                    out_3[g, 4 * q : 4 * q + 4].bitcast(I32), page_s[g][32 * q : 32 * q + 4].bitcast(I32)
+                    out_3[g, SCALE_ROWS * q : SCALE_ROWS * (q + 1)].bitcast(I32),
+                    page_s[g][QUADRANT * q : QUADRANT * q + SCALE_ROWS].bitcast(I32),
                 )
 
-        def collect(c):
-            staged = keep.tile([P, PACK, T2 // 2], F32, name="staged", tag=f"stage{c}")
-            for t in range(PACK):
-                nc.sync.dma_start(staged[:, t, :], page[0][t][:, c * T2 // 2 : (c + 1) * T2 // 2])
-            return staged
-
-        first_w = keep.tile([P, 2 * UNIT], U32, name="first_w", align_bytes=64)
-        first_s = keep.tile([P, 2 * UNIT], U8, name="first_s", align_bytes=64)
-        gather(first_w[:, 0:UNIT], first_s[:, 0:UNIT], 0, 1)
-        gather(first_w[:, UNIT:], first_s[:, UNIT:], 1, 2)
-        quantise_ws(0, nc.vector.tensor_copy, [slots[2][:].bitcast(BF16)[:, 0 : PACK * WS_PART]])
+        early_w = keep.tile([P, S // 2], U32, name="early_w", align_bytes=64)
+        early_s = keep.tile([P, S // 2], U8, name="early_s", align_bytes=64)
+        gather(early_w[:, 0:UNIT], early_s[:, 0:UNIT], 0, 1)
+        gather(early_w[:, UNIT:], early_s[:, UNIT:], 1, 2)
+        ws_woven = scratch[2][:].bitcast(BF16)
+        quantise_ws(0, 0, [ws_woven[:, 0 : PACK * WS_PART]])
         last_pieces = [
-            ring.tile([P, PACK * WS_PART // 2], BF16, name="ws_woven", tag=f"head{i}", bufs=1, align_bytes=64)
-            for i in range(2)
+            ring.tile([P, PACK * WS_PART // 2], BF16, name="ws_piece", tag=f"late{i}", align_bytes=64) for i in range(2)
         ]
-        quantise_ws(1, nc.vector.tensor_copy, [piece[:] for piece in last_pieces])
+        quantise_ws(0, WS_PART, [piece[:] for piece in last_pieces])
         nc.gpsimd.tensor_scalar(scale[:], gain_sb[:], -2.0, 0.0, ALU.mult, ALU.add)
         nc.gpsimd.tensor_scalar(shift[:], gain_sb[:], 2.0, 0.0, ALU.mult, ALU.add)
-        rest_s = ring.tile([P, S // 2], U8, name="rest_s", tag="head1", bufs=1, align_bytes=64)
-        rest_w = ring.tile([P, S // 2], U32, name="rest_w", tag="head0", bufs=1, align_bytes=64)
-        gather(rest_w[:], rest_s[:], 2, 4)
-        v_w = [tile[:, a : a + UNIT] for tile in (first_w, rest_w) for a in (0, UNIT)]
-        v_s = [tile[:, a : a + UNIT] for tile in (first_s, rest_s) for a in (0, UNIT)]
-        unit_of_work(0, 0)
-        late_woven = slots[2][:].bitcast(BF16)
-        quantise_ws(2, nc.vector.tensor_copy, [late_woven[:, 0 : PACK * WS_PART]])
-        quantise_ws(3, nc.vector.tensor_copy, [late_woven[:, PACK * WS_PART :]])
+        late_s = ring.tile([P, S // 2], U8, name="late_s", tag="late1", align_bytes=64)
+        late_w = ring.tile([P, S // 2], U32, name="late_w", tag="late0", align_bytes=64)
+        gather(late_w[:], late_s[:], UNITS // 2, UNITS)
+        v_w = [tile[:, a : a + UNIT] for tile in (early_w, late_w) for a in (0, UNIT)]
+        v_s = [tile[:, a : a + UNIT] for tile in (early_s, late_s) for a in (0, UNIT)]
+
+        unit_of_group_0(0)
+        quantise_ws(1, 0, [ws_woven])
         for u in range(1, UNITS):
-            unit_of_work(0, u)
-        staged = [collect(c) for c in range(2)]
+            unit_of_group_0(u)
+        collected = []
+        for half in range(2):
+            planes = keep.tile([P, PACK, T2 // 2], F32, name="collected", tag=f"stage{half}")
+            for t in range(PACK):
+                nc.sync.dma_start(planes[:, t, :], page[0][t][:, half * T2 // 2 : (half + 1) * T2 // 2])
+            collected.append(planes)
         for t in range(PACK):
             nc.sync.dma_start(page_out[0, t], page[0][t][:])
-        h_more = [keep.tile([P, 2 * UNIT], F32, name=f"h_more{t}") for t in range(PACK)]
-        for u, h_wide in ((0, h_more), (2, h_both)):
-            features(1, u, [h_t[:, 0:UNIT] for h_t in h_wide])
-            if u == 0:
-                scatter(1, 0, 1, 0, h_wide[0][:, 0:UNIT])
-            features(1, u + 1, [h_t[:, UNIT : 2 * UNIT] for h_t in h_wide])
-            for t in range(PACK):
-                if u == 0 and t == 0:
-                    scatter(1, 1, 2, 0, h_wide[0][:, UNIT:])
-                else:
-                    scatter(1, u, u + 2, t, h_wide[t][:])
+
+        features(1, 0, h_sets[1])
+        scatter(1, 0, 1, 0, h_sets[1])
+        features(1, 1, h_sets[1])
+        scatter(1, 1, 2, 0, h_sets[1])
+        for t in range(1, PACK):
+            scatter(1, 0, 2, t, h_sets[1])
+        features(1, 2, h_sets[0])
+        features(1, 3, h_sets[0])
+        for t in range(PACK):
+            scatter(1, 2, UNITS, t, h_sets[0])
+            nc.sync.dma_start(page_out[1, t], page[1][t][:])
+
         for c in range(CHUNKS):
-            woven = ring.tile([P, BANK, PACK], BF16, name="woven", tag="woven", bufs=3, align_bytes=64)
-            weave(nc.vector.tensor_copy if c in (2, 3) else nc.scalar.copy, woven[:], staged[c // 2][:, :, (c % 2) * BANK : (c % 2 + 1) * BANK])
-            quantise_page(0, c, woven[:].rearrange("p c t -> p (c t)"))
+            woven = ring.tile([P, BANK * PACK], BF16, name="woven", tag="woven", bufs=3, align_bytes=64)
+            copy = nc.scalar.copy if c < SCALAR_CHUNKS else nc.vector.tensor_copy
+            interleave(copy, woven[:], collected[c // 2][:, :, (c % 2) * BANK : (c % 2 + 1) * BANK])
+            quantise_page(0, c, woven[:])
         store_scale_rows(0)
 
         pair_tile = keep.tile([P, CHUNKS * 2 * BANK], F32, name="pair_tile", tag="stage0")
         pair_words = [pair_tile[:, c * 2 * BANK : (c + 1) * 2 * BANK] for c in range(CHUNKS)]
-        pairs = [words.bitcast(BF16).rearrange("p (u c e) -> p u c e", u=2, e=2) for words in pair_words]
 
         def round_into_pairs(c, t):
-            nc.scalar.copy(pairs[c][:, t // 2, :, t % 2], page[1][t][:, c * BANK : (c + 1) * BANK])
+            pairs = pair_words[c].bitcast(BF16).rearrange("p (u c e) -> p u c e", u=2, e=2)
+            nc.scalar.copy(pairs[:, t // 2, :, t % 2], page[1][t][:, c * BANK : (c + 1) * BANK])
 
         for t in range(PACK - 1):
             for c in range(CHUNKS):
                 round_into_pairs(c, t)
 
-        banks = args + sums
-
-        def finish_page(c):
+        def finish_chunk(c):
             round_into_pairs(c, PACK - 1)
-            woven = slots[c % len(slots)]
+            woven = scratch[c % len(scratch)]
             nc.scalar.copy(woven[:].rearrange("p (c u) -> p c u", u=2), pair_words[c].rearrange("p (u c) -> p c u", u=2))
             quantise_page(1, c, woven[:].bitcast(BF16))
+
+        banks = args + sums
 
         def alerts(c):
             cols = slice(c * BANK, (c + 1) * BANK)
             for m in range(N_TILES):
-                score = banks[(c * N_TILES + m) % 8]
+                score = banks[(c * N_TILES + m) % len(banks)]
                 for g in range(GROUPS):
                     nc.tensor.matmul_mx(
                         score[:], lhsT=wo_w[:, g * N + m * P : g * N + (m + 1) * P].bitcast(FP8X4),
@@ -295,13 +297,13 @@ def tile_list_ward_page_alerts_kernel(
                         rhs=page_w[g][:, cols].bitcast(FP8X4), rhs_scale=page_s[g][:, cols],
                         start=(g == 0), stop=(g == GROUPS - 1),
                     )
-                nc.vector.tensor_tensor(capped[c][:, m, :], score[:], capped[c][:, m, :], ALU.min)
-                nc.sync.dma_start(out_rows[:, m, cols], capped[c][:, m, :])
+                nc.vector.tensor_tensor(capped[m][:, cols], score[:], capped[m][:, cols], ALU.min)
+                nc.sync.dma_start(out_0[m * P : (m + 1) * P, cols], capped[m][:, cols])
 
-        finish_page(0)
-        for c in range(1, CHUNKS):
-            finish_page(c)
+        for c in range(CHUNKS):
+            finish_chunk(c)
             if c == CHUNKS - 1:
                 store_scale_rows(1)
-            alerts(c - 1)
+            if c > 0:
+                alerts(c - 1)
         alerts(CHUNKS - 1)

import math
from contextlib import ExitStack

import concourse.mybir as mybir
from concourse.masks import make_identity

K, T, S, H, T2, N = 512, 2048, 1024, 1024, 2048, 384
FLOPS = 2 * K * H * S * 2 + 2 * H * N * T2

F32 = mybir.dt.float32
BF16 = mybir.dt.bfloat16
I32 = mybir.dt.int32
U32 = mybir.dt.uint32
U16 = mybir.dt.uint16
U8 = mybir.dt.uint8
FP8X4 = mybir.dt.float8_e4m3fn_x4
FP4X4 = mybir.dt.float4_e2m1fn_x4
ACT = mybir.ActivationFunctionType
ALU = mybir.AluOpType

P = 128
PACK = 4
ROWS = P * PACK
GROUPS = H // ROWS
QUADRANT = 32
SCALE_ROWS = 4
UNIT = 256
UNITS = S // UNIT
LIST_COLS = UNIT // 16
BANK = 512
CHUNKS = T2 // BANK
N_TILES = N // P
WS_PART = 256
NEIGHBOURS = 4
SCALAR_CHUNKS = 2


def tile_list_ward_page_alerts_kernel(
    tc, tab_words, tab_scales, offs, ws, wc_words, wc_scales, gain, page0, offs2, wgs, wo_words, wo_scales, top,
    out_0, out_1, out_2, out_3,
):
    nc = tc.nc
    with ExitStack() as ctx:
        keep = ctx.enter_context(tc.tile_pool(name="keep", bufs=1))
        ring = ctx.enter_context(tc.tile_pool(name="ring", bufs=1))
        psum = ctx.enter_context(tc.psum_pool(name="psum", bufs=1))

        pick = keep.tile([P, S // 16], U16, name="pick")
        place = keep.tile([P, S // 16], U16, name="place")
        tab_w = keep.tile([P, T], U32, name="tab_w")
        tab_s = keep.tile([P, T], U8, name="tab_s")
        wc_w = keep.tile([P, 2 * H], U8, name="wc_w", align_bytes=64)
        wc_s = keep.tile([P, H], U8, name="wc_s", align_bytes=64)
        wo_w = keep.tile([P, GROUPS * N], U32, name="wo_w", align_bytes=64)
        wo_s = keep.tile([P, GROUPS, N], U8, name="wo_s", align_bytes=64)
        nc.vector.memset(tab_s[:].bitcast(I32), 0)
        nc.vector.memset(wc_s[:].bitcast(I32), 0)
        nc.vector.memset(wo_s[:].bitcast(I32), 0)
        ident = keep.tile([P, P], F32, name="ident")
        make_identity(nc, ident[:])

        ws_rows = ws.rearrange("(p t) r -> p t r", t=PACK)
        ws_group = [keep.tile([P, PACK, ROWS], F32, name=f"ws_group{g}", tag=f"stage{g}") for g in range(GROUPS)]
        page_in = page0.rearrange("(g p t) c -> g t p c", g=GROUPS, t=PACK)
        page_out = out_1.rearrange("(g p t) c -> g t p c", g=GROUPS, t=PACK)
        page = [[keep.tile([P, T2], F32, name=f"page{g}{t}") for t in range(PACK)] for g in range(GROUPS)]
        wgs_rows = wgs.rearrange("(q t) j -> q t j", t=PACK)
        factors = [keep.tile([P, PACK, 2 * UNIT], F32, name=f"factors{i}") for i in range(UNITS // 2)]
        gain_sb = keep.tile([P, GROUPS, PACK], F32, name="gain_sb")
        capped = [keep.tile([P, T2], F32, name=f"capped{m}") for m in range(N_TILES)]

        def unit_factors(u0, u1):
            return factors[u0 // 2][:, :, (u0 % 2) * UNIT : (u0 % 2 + u1 - u0) * UNIT]

        def load_scale_rows(queue, scale_tile, rows):
            for q in range(P // QUADRANT):
                queue.dma_start(
                    scale_tile[QUADRANT * q : QUADRANT * q + SCALE_ROWS].bitcast(I32),
                    rows[SCALE_ROWS * q : SCALE_ROWS * (q + 1)].bitcast(I32),
                )

        def load_factors(u0, u1):
            for q in (0, 2, 1, 3):
                nc.sync.dma_start(
                    unit_factors(u0, u1)[QUADRANT * q : QUADRANT * (q + 1)], wgs_rows[:, :, u0 * UNIT : u1 * UNIT]
                )

        nc.sync.dma_start(pick[:], offs)
        nc.sync.dma_start(tab_w[:].bitcast(I32), tab_words[0].rearrange("p t i -> p (t i)").bitcast(I32))
        load_scale_rows(nc.scalar, tab_s, tab_scales[0])
        load_scale_rows(nc.scalar, wc_s, wc_scales[0])
        nc.sync.dma_start(wc_w[:].bitcast(I32), wc_words[0].bitcast(I32))
        for a in range(0, ROWS, WS_PART):
            nc.sync.dma_start(ws_group[0][:, :, a : a + WS_PART], ws_rows[:, :, a : a + WS_PART])
        nc.sync.dma_start(place[:], offs2)
        nc.sync.dma_start(gain_sb[:], gain.rearrange("(g p t) -> p g t", g=GROUPS, t=PACK))
        load_factors(0, 1)
        for t in range(PACK):
            nc.sync.dma_start(page[0][t][:], page_in[0, t])
        nc.sync.dma_start(ws_group[1][:], ws_rows[:, :, ROWS:H])
        load_factors(1, 2)
        load_factors(2, UNITS)
        for t in range(PACK):
            nc.sync.dma_start(page[1][t][:], page_in[1, t])
        nc.sync.dma_start(
            wo_w[:].bitcast(I32).rearrange("p (g n) -> p g n", g=GROUPS),
            wo_words.rearrange("g p n i -> p g (n i)").bitcast(I32),
        )
        load_scale_rows(nc.sync, wo_s, wo_scales.rearrange("g q n -> q g n"))
        for m in range(N_TILES):
            nc.sync.dma_start(capped[m][:], top[m * P : (m + 1) * P, :])

        ws_w = [keep.tile([P, ROWS], U32, name=f"ws_w{g}", align_bytes=64) for g in range(GROUPS)]
        ws_s = [keep.tile([P, ROWS], U8, name=f"ws_s{g}", align_bytes=64) for g in range(GROUPS)]
        page_w = [keep.tile([P, T2], U32, name=f"page_w{g}", align_bytes=64) for g in range(GROUPS)]
        page_s = [keep.tile([P, T2], U8, name=f"page_s{g}", align_bytes=64) for g in range(GROUPS)]
        args = [psum.tile([P, BANK], F32, name=f"args{b}") for b in range(4)]
        sums = [psum.tile([P, BANK], F32, name=f"sums{b}") for b in range(4)]
        scratch = [keep.tile([P, 2 * ROWS], F32, name=f"scratch{b}", align_bytes=64) for b in range(3)]
        scale = keep.tile([P, GROUPS, PACK], F32, name="scale")
        shift = keep.tile([P, GROUPS, PACK], F32, name="shift")
        h_sets = [[keep.tile([P, 2 * UNIT], F32, name=f"h{i}{t}") for t in range(PACK)] for i in range(2)]

        def gather(words, scales, u0, u1):
            entries = pick[:, u0 * LIST_COLS : u1 * LIST_COLS]
            nc.vector.tensor_copy(words, tab_w[:].indirect(entries))
            nc.vector.tensor_copy(scales, tab_s[:].indirect(entries))

        def interleave(copy, woven, planes):
            copy(
                woven.rearrange("p (c i t) -> p c t i", i=NEIGHBOURS, t=PACK),
                planes.rearrange("p t (c i) -> p c t i", i=NEIGHBOURS),
            )

        def quantise_ws(g, first, pieces):
            width = pieces[0].shape[1] // PACK
            spans = [slice(first + i * width, first + (i + 1) * width) for i in range(len(pieces))]
            for woven, cols in zip(pieces, spans):
                interleave(nc.vector.tensor_copy, woven, ws_group[g][:, :, cols])
            for woven, cols in zip(pieces, spans):
                nc.vector.quantize_mx(ws_w[g][:, cols].bitcast(FP8X4), ws_s[g][:, cols], woven)

        def features(g, u, h):
            opening = g == 0 and u == 0
            if opening:
                plane_sums = [sums[t][:, 0:UNIT] for t in range(PACK)]
            else:
                plane_sums = [sums[2 * (u % 2) + t // 2][:, (t % 2) * UNIT : (t % 2 + 1) * UNIT] for t in range(PACK)]
            steps = []
            for s in range(UNIT // P):
                cols = slice(s * P, (s + 1) * P)
                arg_cos, arg_sin = args[2 * s], args[2 * s + 1]
                nc.tensor.matmul_mx(
                    arg_cos[:], lhsT=v_w[u][:, cols].bitcast(FP8X4), lhsT_scale=v_s[u][:, cols],
                    rhs=wc_w[:, 2 * g * ROWS : 2 * (g + 1) * ROWS].bitcast(FP4X4),
                    rhs_scale=wc_s[:, g * ROWS : (g + 1) * ROWS], start=True, stop=True,
                )
                nc.tensor.matmul_mx(
                    arg_sin[:], lhsT=v_w[u][:, cols].bitcast(FP8X4), lhsT_scale=v_s[u][:, cols],
                    rhs=ws_w[g][:].bitcast(FP8X4), rhs_scale=ws_s[g][:], start=True, stop=True,
                )
                halves = scratch[s][:].rearrange("j (a t p) -> j a t p", a=2, t=PACK)
                squares = ring.tile([P, 2, PACK, P], F32, name="squares", tag="squares", bufs=3)
                nc.scalar.activation(
                    halves[:, 0], arg_cos[:].rearrange("j (p t) -> j t p", t=PACK), ACT.Sin, scale=0.5
                )
                if opening:
                    nc.scalar.activation(squares[:, 0], halves[:, 0], ACT.Square)
                nc.scalar.activation(
                    halves[:, 1], arg_sin[:].rearrange("j (p t) -> j t p", t=PACK), ACT.Sin,
                    bias=-math.pi / 4, scale=0.5,
                )
                if opening:
                    nc.scalar.activation(squares[:, 1], halves[:, 1], ACT.Square)
                else:
                    nc.scalar.activation(squares[:], halves, ACT.Square)
                steps.append((cols, squares))
            if opening:
                turns = [(cols, squares, t) for t in range(PACK) for cols, squares in steps]
            else:
                turns = [(cols, squares, t) for cols, squares in steps for t in range(PACK)]
            for cols, squares, t in turns:
                for term in range(2):
                    nc.tensor.matmul(
                        plane_sums[t][:, cols], lhsT=squares[:, term, t, :], rhs=ident[:],
                        start=(term == 0), stop=(term == 1), is_transpose=True,
                    )
            for t in range(PACK):
                nc.scalar.activation(
                    h[t][:, (u % 2) * UNIT : (u % 2 + 1) * UNIT], plane_sums[t], ACT.Identity,
                    bias=shift[:, g, t : t + 1], scale=scale[:, g, t : t + 1],
                )

        def scatter(g, u0, u1, t, h):
            entries = place[:, u0 * LIST_COLS : u1 * LIST_COLS]
            values = h[t][:, (u0 % 2) * UNIT : (u0 % 2 + u1 - u0) * UNIT]
            nc.vector.tensor_tensor(page[g][t][:].indirect(entries), values, unit_factors(u0, u1)[:, t, :], ALU.mult)

        def unit_of_group_0(u):
            features(0, u, h_sets[0])
            for t in range(PACK):
                scatter(0, u, u + 1, t, h_sets[0])

        words_out = out_2.rearrange("g p c i -> g p (c i)")

        def quantise_page(g, c, woven):
            cols = slice(c * BANK, (c + 1) * BANK)
            nc.vector.quantize_mx(page_w[g][:, cols].bitcast(FP8X4), page_s[g][:, cols], woven)
            nc.sync.dma_start(
                words_out[g, :, PACK * c * BANK : PACK * (c + 1) * BANK].bitcast(I32), page_w[g][:, cols].bitcast(I32)
            )

        def store_scale_rows(g):
            for q in range(P // QUADRANT):
                nc.sync.dma_start(
                    out_3[g, SCALE_ROWS * q : SCALE_ROWS * (q + 1)].bitcast(I32),
                    page_s[g][QUADRANT * q : QUADRANT * q + SCALE_ROWS].bitcast(I32),
                )

        early_w = keep.tile([P, S // 2], U32, name="early_w", align_bytes=64)
        early_s = keep.tile([P, S // 2], U8, name="early_s", align_bytes=64)
        gather(early_w[:, 0:UNIT], early_s[:, 0:UNIT], 0, 1)
        gather(early_w[:, UNIT:], early_s[:, UNIT:], 1, 2)
        ws_woven = scratch[2][:].bitcast(BF16)
        quantise_ws(0, 0, [ws_woven[:, 0 : PACK * WS_PART]])
        last_pieces = [
            ring.tile([P, PACK * WS_PART // 2], BF16, name="ws_piece", tag=f"late{i}", align_bytes=64) for i in range(2)
        ]
        quantise_ws(0, WS_PART, [piece[:] for piece in last_pieces])
        nc.gpsimd.tensor_scalar(scale[:], gain_sb[:], -2.0, 0.0, ALU.mult, ALU.add)
        nc.gpsimd.tensor_scalar(shift[:], gain_sb[:], 2.0, 0.0, ALU.mult, ALU.add)
        late_s = ring.tile([P, S // 2], U8, name="late_s", tag="late1", align_bytes=64)
        late_w = ring.tile([P, S // 2], U32, name="late_w", tag="late0", align_bytes=64)
        gather(late_w[:], late_s[:], UNITS // 2, UNITS)
        v_w = [tile[:, a : a + UNIT] for tile in (early_w, late_w) for a in (0, UNIT)]
        v_s = [tile[:, a : a + UNIT] for tile in (early_s, late_s) for a in (0, UNIT)]

        unit_of_group_0(0)
        quantise_ws(1, 0, [ws_woven])
        for u in range(1, UNITS):
            unit_of_group_0(u)
        collected = []
        for half in range(2):
            planes = keep.tile([P, PACK, T2 // 2], F32, name="collected", tag=f"stage{half}")
            for t in range(PACK):
                nc.sync.dma_start(planes[:, t, :], page[0][t][:, half * T2 // 2 : (half + 1) * T2 // 2])
            collected.append(planes)
        for t in range(PACK):
            nc.sync.dma_start(page_out[0, t], page[0][t][:])

        features(1, 0, h_sets[1])
        scatter(1, 0, 1, 0, h_sets[1])
        features(1, 1, h_sets[1])
        scatter(1, 1, 2, 0, h_sets[1])
        for t in range(1, PACK):
            scatter(1, 0, 2, t, h_sets[1])
        features(1, 2, h_sets[0])
        features(1, 3, h_sets[0])
        for t in range(PACK):
            scatter(1, 2, UNITS, t, h_sets[0])
            nc.sync.dma_start(page_out[1, t], page[1][t][:])

        for c in range(CHUNKS):
            woven = ring.tile([P, BANK * PACK], BF16, name="woven", tag="woven", bufs=3, align_bytes=64)
            copy = nc.scalar.copy if c < SCALAR_CHUNKS else nc.vector.tensor_copy
            interleave(copy, woven[:], collected[c // 2][:, :, (c % 2) * BANK : (c % 2 + 1) * BANK])
            quantise_page(0, c, woven[:])
        store_scale_rows(0)

        pair_tile = keep.tile([P, CHUNKS * 2 * BANK], F32, name="pair_tile", tag="stage0")
        pair_words = [pair_tile[:, c * 2 * BANK : (c + 1) * 2 * BANK] for c in range(CHUNKS)]

        def round_into_pairs(c, t):
            pairs = pair_words[c].bitcast(BF16).rearrange("p (u c e) -> p u c e", u=2, e=2)
            nc.scalar.copy(pairs[:, t // 2, :, t % 2], page[1][t][:, c * BANK : (c + 1) * BANK])

        for t in range(PACK - 1):
            for c in range(CHUNKS):
                round_into_pairs(c, t)

        def finish_chunk(c):
            round_into_pairs(c, PACK - 1)
            woven = scratch[c % len(scratch)]
            nc.scalar.copy(woven[:].rearrange("p (c u) -> p c u", u=2), pair_words[c].rearrange("p (u c) -> p c u", u=2))
            quantise_page(1, c, woven[:].bitcast(BF16))

        banks = args + sums

        def alerts(c):
            cols = slice(c * BANK, (c + 1) * BANK)
            for m in range(N_TILES):
                score = banks[(c * N_TILES + m) % len(banks)]
                for g in range(GROUPS):
                    nc.tensor.matmul_mx(
                        score[:], lhsT=wo_w[:, g * N + m * P : g * N + (m + 1) * P].bitcast(FP8X4),
                        lhsT_scale=wo_s[:, g, m * P : (m + 1) * P],
                        rhs=page_w[g][:, cols].bitcast(FP8X4), rhs_scale=page_s[g][:, cols],
                        start=(g == 0), stop=(g == GROUPS - 1),
                    )
                nc.vector.tensor_tensor(capped[m][:, cols], score[:], capped[m][:, cols], ALU.min)
                nc.sync.dma_start(out_0[m * P : (m + 1) * P, cols], capped[m][:, cols])

        for c in range(CHUNKS):
            finish_chunk(c)
            if c == CHUNKS - 1:
                store_scale_rows(1)
            if c > 0:
                alerts(c - 1)
        alerts(CHUNKS - 1)
